import numpy as np
import ml_dtypes


def mxq(x, axis, fmt="e4m3"):
    dtype, down = {"e4m3": (ml_dtypes.float8_e4m3fn, 7), "e5m2": (ml_dtypes.float8_e5m2, 14)}[fmt]
    v = np.moveaxis(np.asarray(x, np.float32).astype(ml_dtypes.bfloat16).astype(np.float64), axis, -1)
    blocks = v.reshape(v.shape[:-1] + (-1, 32))
    amax = np.abs(blocks).max(-1, keepdims=True)
    byte = np.maximum(np.where(amax > 0, np.frexp(amax)[1] - 1 + 127, 0) - down, 1)
    scale = np.exp2(byte - 127.0)
    codes = (blocks / scale).astype(np.float32).astype(dtype).astype(np.float64)
    return np.moveaxis((codes * scale).reshape(v.shape), -1, axis)


WIDE = False


def mx_kscale(k):
    if not WIDE:
        return np.ones(k)
    levels = np.array([10, -10, 5, -5, 0])
    if k % 512:
        return np.exp2(np.random.permutation(np.resize(levels, k // 32))).repeat(32)
    a = np.empty((k // 512, 16))
    for p in range(k // 512):
        a[p, :8] = np.random.permutation(np.resize(levels, 8))
        for g in range(8):
            far = levels[np.abs(levels - a[p, g]) >= 10]
            a[p, g + 8] = far[np.random.randint(len(far))]
    return np.exp2(a.ravel()).repeat(32)


BF16 = ml_dtypes.bfloat16


def bf(x):
    return np.asarray(x, np.float32).astype(BF16)


def f64(x):
    return np.asarray(x).astype(np.float64)


E2M1 = np.array([0.0, 0.5, 1.0, 1.5, 2.0, 3.0, 4.0, 6.0, -0.0, -0.5, -1.0, -1.5, -2.0, -3.0, -4.0, -6.0])


def pack_weight(w, fmt):
    k, n = w.shape
    w = f64(bf(w)).reshape(k // 32, 32, n)
    amax = np.abs(w).max(1)
    if fmt == "e4m3":
        byte = np.frexp(amax)[1] - 1 + 127 - 7
    else:
        mant, ex = np.frexp(amax / 6.0)
        byte = np.where(mant > 0.5, ex, ex - 1) + 127
    byte = np.clip(np.where(amax > 0, byte, 1), 1, 254)
    scaled = (w * np.exp2(127.0 - byte)[:, None, :]).reshape(k, n).astype(np.float32)
    by_word = np.ascontiguousarray(scaled.reshape(k // 512, 128, 4, n).transpose(0, 1, 3, 2))
    if fmt == "e4m3":
        words = by_word.astype(ml_dtypes.float8_e4m3fn).view(np.uint8)
    else:
        c = by_word.astype(ml_dtypes.float4_e2m1fn).view(np.uint8) & 0xF
        words = c[..., 0::2] | (c[..., 1::2] << 4)
    return np.ascontiguousarray(words), np.ascontiguousarray(byte.astype(np.uint8).reshape(k // 512, 16, n))


def unpack_weight(words, scales, fmt):
    g, p, n, _ = words.shape
    if fmt == "e4m3":
        vals = np.ascontiguousarray(words).view(ml_dtypes.float8_e4m3fn).astype(np.float64)
    else:
        nib = np.empty((g, p, n, 4), np.uint8)
        nib[..., 0::2] = words & 0xF
        nib[..., 1::2] = words >> 4
        vals = E2M1[nib]
    vals = vals * np.repeat(np.exp2(scales.astype(np.float64) - 127.0), 8, axis=1)[..., None]
    return vals.transpose(0, 1, 3, 2).reshape(g * 512, n)
def pack4(w):
    words, scales = pack_weight(w, "e2m1")
    return words.reshape(words.shape[0], 128, -1), scales


def unpack4(words, scales):
    return unpack_weight(words.reshape(words.shape[0], 128, -1, 2), scales, "e2m1")


M, F, N = 1024, 2048, 1024
SLOPE = 0.25


def setup_inputs():
    s = mx_kscale(F)
    t = mx_kscale(F)
    z = np.random.standard_normal((M, F)) * t
    dz = np.random.standard_normal((M, F)) * s
    w2_words, w2_scales = pack4(np.random.standard_normal((F, N)) / np.sqrt(F) / s[:, None])
    v2 = np.random.standard_normal((F, N)) / np.sqrt(F) / t[:, None]
    vb = 0.3 * np.random.standard_normal(N)
    c = np.random.uniform(0.5, 1.5, (M, N))
    return {"z": bf(z), "dz": bf(dz), "w2_words": w2_words, "w2_scales": w2_scales,
            "v2": bf(v2), "vb": bf(vb), "c": bf(c)}


def reference(z, dz, w2_words, w2_scales, v2, vb, c):
    zf = f64(z)
    d = np.where(zf > 0, 1.0, SLOPE)
    h = zf * d
    dh = f64(dz) * d
    through = mxq(dh, 1, "e4m3") @ unpack4(w2_words, w2_scales)
    direct = mxq(h, 1, "e4m3") @ mxq(f64(v2), 0, "e4m3")
    jv = through + direct + f64(vb)
    return jv * f64(c)

@@ -1,0 +1,294 @@
+from contextlib import ExitStack
+
+import concourse.mybir as mybir
+from concourse.masks import make_identity
+
+M, F, N = 1024, 2048, 1024
+SLOPE = 0.25
+FLOPS = 2 * 2 * M * F * N
+
+F32 = mybir.dt.float32
+BF16 = mybir.dt.bfloat16
+I32 = mybir.dt.int32
+U32 = mybir.dt.uint32
+U8 = mybir.dt.uint8
+FP8X4 = mybir.dt.float8_e4m3fn_x4
+FP4X4 = mybir.dt.float4_e2m1fn_x4
+ALU = mybir.AluOpType
+
+P = 128
+PASSES = F // 512
+HALF = 512
+TILES = M // P
+BANKS = 4
+
+EARLY = (1, 2, 3, 4)
+
+SYNC = """
+lz0 lz1 ldz0 lz2 ldz1 ldz2 lb lv00 lz3 lv10 ldz3 lz4 lw0 lz5 lv20 ldz4 lv30 lv01 lv11 lz6 lw1 ldz5 lv21
+lz7 lv31 lc0 ldz6 ldz7 lc1 lc2 lc3 lc4 lc5 lc6 lc7 st00 st10 st20 st30 st40 st01 st11 st21 st31 st41
+st50 st51 st60 st61 st70 st71
+"""
+VECTOR = """
+d0 h0 dh0 d1 h1 Qh0 d2 dh1 dh2 Qh1 Qdh1 Qv00 h2 Qdh2 d3 Qdh0 Qh2 dh3 Qv10 h3 Qdh3 d4 Qh3 d5 h4 Qv20
+h5 Qh4 Qv30 dh4 d6 Qdh4 A00 dh5 A10 Qv01 A20 h6 A30 d7 Qv11 A40 h7 Qh5 Qv21 dh6 Qdh5 Qv31 dh7 X00
+A01 Qh6 A11 Qdh6 A21 X10 A31 Qh7 X20 Qdh7 X30 A41 X40 X01 A50 X11 X21 A51 X31 X41 A60 X50 X51 A61
+X60 X61 A70 A71 X70 X71
+"""
+SCALAR = """
+Eh1 Eh0 Eh2 I00 Edh0 b0 Eh3 I10 Eh4 b1 I20 I30 I01 Eh5 I11 Edh5 I21 Eh6 I31 Edh6 Eh7 Edh7
+"""
+TENSOR = """
+Th1 Th0 Th2 Tdh1 Tdh2 Tdh0 B0 Th3 Tdh3 M00v0 M10v0 Th4 B1 M20v0 M00w M10w M20w M00v1 M10v1 M20v1 Tdh4 M30w
+M30v0 M30v1 M00v2 M10v2 M20v2 M30v2 M00v3 M10v3 M20v3 M30v3 Th5 M40 Tdh5 M01w M11w Th6 M21w M01v0
+M11v0 M21v0 M31w M31v0 M01v1 M11v1 M21v1 M31v1 M01v2 M11v2 M21v2 M31v2 Tdh6 Th7 M01v3 M11v3 M21v3
+M31v3 M41 Tdh7 M50 M51 M60 M61 M70 M71
+"""
+
+
+def expand(text):
+    steps = []
+    for word in text.split():
+        if word[0] == "M":
+            kinds = word[3:4] or "wv"
+            passes = word[4:5] or "0123"
+            steps.extend(word[:3] + kind + g for kind in kinds for g in passes)
+        elif word[0] in "TE" or (word.startswith("dh") and int(word[2]) in EARLY):
+            steps.extend([word + "0", word + "1"])
+        else:
+            steps.append(word)
+    return steps
+
+
+def tile_gauss_newton_output_side_s1_kernel(tc, z, dz, w2_words, w2_scales, v2, vb, c, out):
+    nc = tc.nc
+    with ExitStack() as ctx:
+        keep = ctx.enter_context(tc.tile_pool(name="keep", bufs=1))
+        work = ctx.enter_context(tc.tile_pool(name="work", bufs=1))
+        psum = ctx.enter_context(tc.psum_pool(name="psum", bufs=1))
+        ctx.enter_context(tc.manual_schedule())
+
+        ident = keep.tile([P, P], F32, name="ident")
+        vb_rows = keep.tile([P, P], F32, name="vb_rows")
+        vb_cols = keep.tile([P, 4], F32, name="vb_cols")
+        vb_all = keep.tile([P, N], BF16, name="vb_all")
+        w_scales = keep.tile([P, PASSES, N], U8, name="w_scales", align_bytes=64)
+        make_identity(nc, ident[:])
+        nc.gpsimd.memset(vb_rows[:], 0.0)
+        nc.gpsimd.memset(w_scales[:].bitcast(I32), 0)
+
+        t = {}
+        turn = {"t": [], "a": []}
+
+        def bank(kind, key):
+            turn[kind].append(key)
+            tag = "%s%d" % (kind, (len(turn[kind]) - 1) % BANKS)
+            t[key] = psum.tile([P, 512], F32, name=tag, tag=tag)
+            return t[key]
+
+        def paired(ap):
+            return ap.rearrange("p (w u e) -> p u w e", u=2, e=2)
+
+        def split(ap):
+            return ap.rearrange("p (u w e) -> p u w e", u=2, e=2)
+
+        def k_tile(key):
+            if key not in t:
+                t[key] = work.tile([P, F], BF16, name="kt", tag="kt", bufs=6, align_bytes=64)
+            return t[key]
+
+        def freed():
+            if len(turn["t"]) < BANKS:
+                return []
+            old = turn["t"][-BANKS]
+            if old[0] == "B":
+                return ["b" + old[1]]
+            early_dh = old.startswith("Tdh") and int(old[-2]) in EARLY
+            return [old[1:] if early_dh else "E" + old[1:]]
+
+        def needs(step):
+            if step.startswith("lz") or step.startswith("ldz"):
+                i = int(step[-1]) - 4
+                if i < 0:
+                    return []
+                s = "h" if step.startswith("lz") else "dh"
+                return ["T%s%d1" % (s, i)] if i in EARLY else ["%s%d" % (s, i)]
+            if step[0] == "l":
+                return []
+            if step[0] == "B":
+                return [{"0": "lb", "1": "b0"}[step[1]]] + freed()
+            if step[0] == "b":
+                return ["B" + step[1]]
+            if step.startswith("st"):
+                return ["X" + step[2:]]
+            if step[0] == "X":
+                return ["A" + step[1:], "lc" + step[1]]
+            if step[0] == "A":
+                return ["b1"] + ["M" + step[1:] + kind + g for kind in "wv" for g in "0123"]
+            if step[0] == "M":
+                need = ["Qdh" + step[1], "lw" + step[2]] if step[3] == "w" else ["Qh" + step[1], "Qv" + step[4] + step[2]]
+                if "M" + step[1:3] not in t and len(turn["a"]) >= BANKS:
+                    need.append("A" + turn["a"][-BANKS][1:])
+                return need
+            if step.startswith("Qv"):
+                return ["I" + step[2:]]
+            if step[0] == "I":
+                return ["lv" + step[1:]]
+            if step[0] == "Q":
+                s, i = step[1:-1], step[-1]
+                if int(i) not in EARLY:
+                    return ["E" + s + i + "0", "E" + s + i + "1"]
+                return ["h" + i] if s == "h" else ["dh" + i + "0", "dh" + i + "1"]
+            if step[0] == "E":
+                return ["T" + step[1:]]
+            if step[0] == "T":
+                s, i = step[1:-2], step[-2]
+                need = [{"h": "lz", "dh": "ldz"}[s] + i] if int(i) in EARLY else [s + i]
+                return need + freed()
+            if step.startswith("dh"):
+                i = step[2]
+                return ["d" + i, "T" + step] if int(i) in EARLY else ["d" + i, "ldz" + i]
+            if step[0] == "h":
+                return ["d" + step[1]]
+            i = step[1]
+            return ["Eh" + i + "0", "Eh" + i + "1"] if int(i) in EARLY else ["lz" + i]
+
+        def emit(step):
+            if step.startswith("lz") or step.startswith("ldz"):
+                i = int(step[-1])
+                src = z if step.startswith("lz") else dz
+                t[step] = work.tile([P, F], BF16, name=step[:-1], tag=step[:-1], bufs=4)
+                nc.sync.dma_start(out=t[step][:], in_=src[i * P : (i + 1) * P, :])
+            elif step == "lb":
+                nc.sync.dma_start(out=vb_rows[0:4, :], in_=vb.bitcast(F32).rearrange("(j p) -> j p", p=P))
+            elif step == "B0":
+                nc.tensor.transpose(bank("t", step)[:, 0:P], vb_rows[:], ident[:])
+            elif step == "b0":
+                nc.scalar.copy(out=vb_cols[:], in_=t["B0"][:, 0:4])
+            elif step == "B1":
+                dst = bank("t", step)
+                for j in range(4):
+                    nc.tensor.transpose(dst[:, j * P : (j + 1) * P], vb_cols[:, j : j + 1].to_broadcast([P, P]), ident[:])
+            elif step == "b1":
+                nc.scalar.copy(out=vb_all[:].bitcast(F32), in_=t["B1"][:])
+            elif step.startswith("lc"):
+                i = int(step[2])
+                t[step] = keep.tile([P, N], BF16, name=step)
+                nc.sync.dma_start(out=t[step][:], in_=c[i * P : (i + 1) * P, :])
+            elif step.startswith("lv"):
+                g, n = int(step[2]), int(step[3])
+                t[step] = work.tile([P, 4, HALF], BF16, name="lv", tag="lv", bufs=4)
+                rows = v2[g * 512 : (g + 1) * 512, n * HALF : (n + 1) * HALF]
+                nc.sync.dma_start(out=t[step][:], in_=rows.rearrange("(p j) n -> p j n", j=4))
+            elif step.startswith("lw"):
+                n = int(step[2])
+                if n == 0:
+                    for q in range(4):
+                        rows = w2_scales[:, 4 * q : 4 * q + 4, :].rearrange("g r n -> r g n")
+                        nc.sync.dma_start(out=w_scales[32 * q : 32 * q + 4, :, :].bitcast(I32), in_=rows.bitcast(I32))
+                t[step] = keep.tile([P, PASSES, 2 * HALF], U8, name=step, align_bytes=64)
+                words = w2_words[:, :, 2 * HALF * n : 2 * HALF * (n + 1)].rearrange("g p b -> p g b")
+                nc.sync.dma_start(out=t[step][:].bitcast(I32), in_=words.bitcast(I32))
+            elif step.startswith("st"):
+                i, n = int(step[2]), int(step[3])
+                nc.sync.dma_start(out=out[i * P : (i + 1) * P, n * HALF : (n + 1) * HALF], in_=t["A" + step[2:]][:])
+            elif step[0] == "X":
+                n = int(step[2])
+                o = t["A" + step[1:]]
+                nc.vector.tensor_tensor(out=o[:], in0=o[:], in1=t["lc" + step[1]][:, n * HALF : (n + 1) * HALF], op=ALU.mult)
+            elif step[0] == "A":
+                n = int(step[2])
+                t[step] = work.tile([P, HALF], F32, name="res", tag="res", bufs=10)
+                nc.vector.tensor_tensor(
+                    out=t[step][:], in0=t["M" + step[1:]][:], in1=vb_all[:, n * HALF : (n + 1) * HALF], op=ALU.add
+                )
+            elif step[0] == "M":
+                key, n, g = step[:3], int(step[2]), int(step[4])
+                opening = key not in t
+                acc = bank("a", key) if opening else t[key]
+                t[key + "count"] = t.get(key + "count", 0) + 1
+                codes, scales = t[("Qdh" if step[3] == "w" else "Qh") + step[1]]
+                if step[3] == "w":
+                    rhs = t["lw" + step[2]][:, g, :].bitcast(FP4X4)
+                    rhs_scale = w_scales[:, g, n * HALF : (n + 1) * HALF]
+                else:
+                    v_codes, v_scales = t["Qv" + step[4] + step[2]]
+                    rhs, rhs_scale = v_codes[:].bitcast(FP8X4), v_scales[:]
+                nc.tensor.matmul_mx(
+                    out=acc[:],
+                    lhsT=codes[:, g * P : (g + 1) * P].bitcast(FP8X4),
+                    lhsT_scale=scales[:, g * P : (g + 1) * P],
+                    rhs=rhs,
+                    rhs_scale=rhs_scale,
+                    start=opening,
+                    stop=t[key + "count"] == 2 * PASSES,
+                )
+            elif step[0] == "Q":
+                src = t["I" + step[2:]] if step[1] == "v" else t["k" + step[1:]]
+                codes = keep.tile([P, 512], U32, name=step + "codes", align_bytes=64)
+                scales = keep.tile([P, 512], U8, name=step + "scales", align_bytes=64)
+                t[step] = (codes, scales)
+                nc.vector.quantize_mx(out=codes[:].bitcast(FP8X4), scales=scales[:], in_=src[:])
+            elif step[0] == "I":
+                t[step] = work.tile([P, 4 * HALF], BF16, name="vi", tag="vi", bufs=3, align_bytes=64)
+                nc.scalar.copy(
+                    out=t[step][:].rearrange("p (c i j) -> p c j i", i=4, j=4),
+                    in_=t["lv" + step[1:]][:].rearrange("p j (c i) -> p c j i", i=4),
+                )
+            elif step[0] == "E":
+                j = int(step[-1])
+                words = k_tile("k" + step[1:-1])[:].bitcast(F32)[:, j * 512 : (j + 1) * 512]
+                nc.scalar.copy(
+                    out=words.rearrange("p (r u) -> p r u", u=2),
+                    in_=t["T" + step[1:]][:].rearrange("p (u r) -> p r u", u=2),
+                )
+            elif step[0] == "T":
+                s, i, j = step[1:-2], step[-2], int(step[-1])
+                dst = bank("t", step)
+                for gg in range(2):
+                    g = 2 * j + gg
+                    for u in range(2):
+                        if int(i) in EARLY:
+                            words = t[{"h": "lz", "dh": "ldz"}[s] + i][:].bitcast(F32)
+                            src = words[:, 256 * g + u : 256 * (g + 1) : 2]
+                        else:
+                            words = t[s + i][:].bitcast(F32)
+                            src = words[:, 512 * u + P * g : 512 * u + P * (g + 1)]
+                        nc.tensor.transpose(dst[:, 256 * u + P * gg : 256 * u + P * (gg + 1)], src, ident[:])
+            elif step.startswith("dh") and int(step[2]) in EARLY:
+                i, j = step[2], int(step[3])
+                cols = slice(j * 1024, (j + 1) * 1024)
+                nc.vector.tensor_tensor(
+                    out=k_tile("kdh" + i)[:, cols].rearrange("p (r u e) -> p r u e", u=2, e=2),
+                    in0=t["T" + step][:].bitcast(BF16).rearrange("p (u r e) -> p r u e", u=2, e=2),
+                    in1=t["d" + i][:, cols].rearrange("p (r u e) -> p r u e", u=2, e=2),
+                    op=ALU.mult,
+                )
+            elif step[0] == "h" and int(step[1]) in EARLY:
+                kt = t["kh" + step[1]]
+                nc.vector.tensor_tensor(out=kt[:], in0=kt[:], in1=t["d" + step[1]][:], op=ALU.mult)
+            elif step[0] == "h" or step.startswith("dh"):
+                i = step[-1]
+                src = t[("lz" if step[0] == "h" else "ldz") + i]
+                t[step] = work.tile([P, F], BF16, name="perm", tag="perm", bufs=3)
+                nc.vector.tensor_tensor(out=split(t[step][:]), in0=paired(src[:]), in1=split(t["d" + i][:]), op=ALU.mult)
+            else:
+                i = step[1]
+                t[step] = work.tile([P, F], BF16, name="slope", tag="slope", bufs=3)
+                if int(i) in EARLY:
+                    dst, src = t[step][:], t["kh" + i][:]
+                else:
+                    dst, src = split(t[step][:]), paired(t["lz" + i][:])
+                nc.vector.tensor_scalar(out=dst, in0=src, scalar1=0.0, scalar2=SLOPE, op0=ALU.is_gt, op1=ALU.max)
+
+        queues = [expand(text) for text in (TENSOR, SCALAR, VECTOR, SYNC)]
+        at = [0] * len(queues)
+        done = set()
+        while len(done) < sum(len(q) for q in queues):
+            before = len(done)
+            for e, q in enumerate(queues):
+                if at[e] < len(q) and all(n in done for n in needs(q[at[e]])):
+                    emit(q[at[e]])
+                    done.add(q[at[e]])
+                    at[e] += 1
+            assert len(done) > before

@@ -17,32 +17,31 @@ FP4X4 = mybir.dt.float4_e2m1fn_x4
 ALU = mybir.AluOpType
 
 P = 128
-PASSES = F // 512
+K_PASS = 512
+PASSES = F // K_PASS
 HALF = 512
-TILES = M // P
 BANKS = 4
+C_TILES = 4
+LAST = "7"
 
-EARLY = (1, 2, 3, 4)
+RAW = "234"
 
 SYNC = """
-lz0 lz1 ldz0 lz2 ldz1 ldz2 lb lv00 lz3 lv10 ldz3 lz4 lw0 lz5 lv20 ldz4 lv30 lv01 lv11 lz6 lw1 ldz5 lv21
-lz7 lv31 lc0 ldz6 ldz7 lc1 lc2 lc3 lc4 lc5 lc6 lc7 st00 st10 st20 st30 st40 st01 st11 st21 st31 st41
-st50 st51 st60 st61 st70 st71
+lz0 lz2 lb ldz0 lz1 ldz1 lz3 lw0 ldz2 lv00 ldz3 lv10 lz4 lv20 ldz4 lv30 lv01 lz5 lv11 lw1 ldz5 lv21
+lz6 lv31 ldz6 lz7 ldz7 lc0 lc1 sw0 sw1 sw2 sw3 sw4 st60 st61 sw5 st70 st71 st72
 """
 VECTOR = """
-d0 h0 dh0 d1 h1 Qh0 d2 dh1 dh2 Qh1 Qdh1 Qv00 h2 Qdh2 d3 Qdh0 Qh2 dh3 Qv10 h3 Qdh3 d4 Qh3 d5 h4 Qv20
-h5 Qh4 Qv30 dh4 d6 Qdh4 A00 dh5 A10 Qv01 A20 h6 A30 d7 Qv11 A40 h7 Qh5 Qv21 dh6 Qdh5 Qv31 dh7 X00
-A01 Qh6 A11 Qdh6 A21 X10 A31 Qh7 X20 Qdh7 X30 A41 X40 X01 A50 X11 X21 A51 X31 X41 A60 X50 X51 A61
-X60 X61 A70 A71 X70 X71
+Z d0 h0 dh0 d1 h1 dh1 Qh0 d2 Qdh0 h2 Qb1 dh2 d3 Qb2 Qv00 h3 dh3 Qv10 d4 Qb3 dh4 Qv20 h4 Qv30 Qb4 A00
+Qv01 A10 d5 A20 A30 Qv11 A40 hd5 d6 Qv21 d7 Qv31 hd6 hd7 A01 A11 Qb5 A21 Y0 Y1 A31 A41 Y2 Qb6 A50 Y3
+Y4 Qb7 A60 X60 A51 A61 Y5 X61 A70 X70 A71 A72 X71 X72
 """
 SCALAR = """
-Eh1 Eh0 Eh2 I00 Edh0 b0 Eh3 I10 Eh4 b1 I20 I30 I01 Eh5 I11 Edh5 I21 Eh6 I31 Edh6 Eh7 Edh7
+Eh0 Edh0 Eh2 b0 Eh1 Edh1 Eh3 b1 I00 I10 Eh4 I20 I30 I01 I11 I21 I31 Eb5 Eb6 Eb7
 """
 TENSOR = """
-Th1 Th0 Th2 Tdh1 Tdh2 Tdh0 B0 Th3 Tdh3 M00v0 M10v0 Th4 B1 M20v0 M00w M10w M20w M00v1 M10v1 M20v1 Tdh4 M30w
-M30v0 M30v1 M00v2 M10v2 M20v2 M30v2 M00v3 M10v3 M20v3 M30v3 Th5 M40 Tdh5 M01w M11w Th6 M21w M01v0
-M11v0 M21v0 M31w M31v0 M01v1 M11v1 M21v1 M31v1 M01v2 M11v2 M21v2 M31v2 Tdh6 Th7 M01v3 M11v3 M21v3
-M31v3 M41 Tdh7 M50 M51 M60 M61 M70 M71
+W2 W2 W2 Th0 W2 Tdh0 Th2 B0 W2 Th1 Tdh1 W2 Th3 B1 W2 Tdh2 M0:0w Tdh3 M1:0w Th4 M012:0v0 M2:0w Tdh4
+M3:0w M0123:0v1 M3:0v0 M0123:0v2 M0123:0v3 M4:0 M0:1w M1:1w M012:1v0 M2:1w Tb5 M3:1w M3:1v0
+M0123:1v1 M0123:1v2 M0123:1v3 Tb6 M4:1 Tb7 M5:0 M5:1 M6:0 M6:1 M7:0 M7:1
 """
 
 
@@ -50,14 +49,26 @@ def expand(text):
     steps = []
     for word in text.split():
         if word[0] == "M":
-            kinds = word[3:4] or "wv"
-            passes = word[4:5] or "0123"
-            steps.extend(word[:3] + kind + g for kind in kinds for g in passes)
-        elif word[0] in "TE" or (word.startswith("dh") and int(word[2]) in EARLY):
+            tiles, rest = word[1:].split(":")
+            kinds = rest[1:2] or "wv"
+            passes = rest[2:3] or "0123"
+            steps.extend("M" + i + rest[0] + kind + g for i in tiles for kind in kinds for g in passes)
+        elif word[0] == "W":
+            steps.extend("W%d.%d" % (len(steps), k) for k in range(int(word[1:])))
+        elif word[:2] in ("Tb", "Eb"):
+            steps.extend(word[0] + s + word[2] + j for s in ("h", "dh") for j in "01")
+        elif word[0] in "TE" or (word.startswith("dh") and word[2] in RAW):
             steps.extend([word + "0", word + "1"])
         else:
             steps.append(word)
     return steps
+
+
+def columns(i, n):
+    if i == LAST and n != "0":
+        first = HALF + (int(n) - 1) * (HALF // 2)
+        return slice(first, first + HALF // 2)
+    return slice(int(n) * HALF, (int(n) + 1) * HALF)
 
 
 def tile_gauss_newton_output_side_s1_kernel(tc, z, dz, w2_words, w2_scales, v2, vb, c, out):
@@ -77,8 +88,11 @@ def tile_gauss_newton_output_side_s1_kernel(tc, z, dz, w2_words, w2_scales, v2, 
         nc.gpsimd.memset(vb_rows[:], 0.0)
         nc.gpsimd.memset(w_scales[:].bitcast(I32), 0)
 
+        queues = [expand(text) for text in (TENSOR, SCALAR, VECTOR, SYNC)]
+        every = [step for queue in queues for step in queue]
+        side = {"h": 0, "dh": 1}
         t = {}
-        turn = {"t": [], "a": []}
+        turn = {"turn": [], "sum": []}
 
         def bank(kind, key):
             turn[kind].append(key)
@@ -86,100 +100,98 @@ def tile_gauss_newton_output_side_s1_kernel(tc, z, dz, w2_words, w2_scales, v2, 
             t[key] = psum.tile([P, 512], F32, name=tag, tag=tag)
             return t[key]
 
-        def paired(ap):
-            return ap.rearrange("p (w u e) -> p u w e", u=2, e=2)
+        def shared(tag, i, shape, dtype, bufs):
+            if tag + i not in t:
+                t[tag + i] = work.tile(shape, dtype, name=tag, tag=tag, bufs=bufs, align_bytes=64)
+            return t[tag + i]
 
-        def split(ap):
-            return ap.rearrange("p (u w e) -> p u w e", u=2, e=2)
+        def raw_rows(i):
+            return shared("rows", i, [P, 2, F], BF16, 5)
 
-        def k_tile(key):
+        def k_tile(i):
+            return shared("ktile", i, [P, 2, F], BF16, 4)
+
+        def parted(i):
+            return shared("parted", i, [P, 2, 2, F // 2], BF16, 2)
+
+        def quantised(key, width):
             if key not in t:
-                t[key] = work.tile([P, F], BF16, name="kt", tag="kt", bufs=6, align_bytes=64)
+                codes = keep.tile([P, width], U32, name=key + "codes", align_bytes=64)
+                scales = keep.tile([P, width], U8, name=key + "scales", align_bytes=64)
+                t[key] = (codes, scales)
             return t[key]
 
+        def among(*steps):
+            return [step for step in steps if step in every]
+
         def freed():
-            if len(turn["t"]) < BANKS:
+            if len(turn["turn"]) < BANKS:
                 return []
-            old = turn["t"][-BANKS]
-            if old[0] == "B":
-                return ["b" + old[1]]
-            early_dh = old.startswith("Tdh") and int(old[-2]) in EARLY
-            return [old[1:] if early_dh else "E" + old[1:]]
+            old = turn["turn"][-BANKS]
+            return among("b" + old[1:], "E" + old[1:], old[1:])
 
         def needs(step):
-            if step.startswith("lz") or step.startswith("ldz"):
-                i = int(step[-1]) - 4
-                if i < 0:
-                    return []
-                s = "h" if step.startswith("lz") else "dh"
-                return ["T%s%d1" % (s, i)] if i in EARLY else ["%s%d" % (s, i)]
-            if step[0] == "l":
+            if step[0] == "l" or step == "Z":
                 return []
+            if step[0] == "W":
+                return ["Z"]
             if step[0] == "B":
                 return [{"0": "lb", "1": "b0"}[step[1]]] + freed()
             if step[0] == "b":
                 return ["B" + step[1]]
-            if step.startswith("st"):
-                return ["X" + step[2:]]
-            if step[0] == "X":
-                return ["A" + step[1:], "lc" + step[1]]
+            if step[0] == "s":
+                return among("X" + step[2:], "Y" + step[2:])
+            if step[0] in "XY":
+                i = step[1]
+                return ["lc%d" % (int(i) // C_TILES)] + (["A" + step[1:]] if step[0] == "X" else ["A" + i + "0", "A" + i + "1"])
             if step[0] == "A":
-                return ["b1"] + ["M" + step[1:] + kind + g for kind in "wv" for g in "0123"]
+                key = "M" + step[1] + min(step[2], "1")
+                return ["b1"] + [key + kind + g for kind in "wv" for g in "0123"]
             if step[0] == "M":
-                need = ["Qdh" + step[1], "lw" + step[2]] if step[3] == "w" else ["Qh" + step[1], "Qv" + step[4] + step[2]]
-                if "M" + step[1:3] not in t and len(turn["a"]) >= BANKS:
-                    need.append("A" + turn["a"][-BANKS][1:])
+                i, n, kind, g = step[1:]
+                need = among("Qb" + i, "Qdh" + i) + ["lw" + n] if kind == "w" else among("Qb" + i, "Qh" + i) + ["Qv" + g + n]
+                if step[:3] not in t and len(turn["sum"]) >= BANKS:
+                    need.append("A" + turn["sum"][-BANKS][1:])
                 return need
             if step.startswith("Qv"):
                 return ["I" + step[2:]]
             if step[0] == "I":
                 return ["lv" + step[1:]]
             if step[0] == "Q":
-                s, i = step[1:-1], step[-1]
-                if int(i) not in EARLY:
-                    return ["E" + s + i + "0", "E" + s + i + "1"]
-                return ["h" + i] if s == "h" else ["dh" + i + "0", "dh" + i + "1"]
+                i = step[-1]
+                sides = ("h", "dh") if step[1] == "b" else (step[1:-1],)
+                makers = [s + i + j for s in sides for j in ("", "0", "1")]
+                return among(*makers) if i in RAW else among(*["E" + maker for maker in makers])
             if step[0] == "E":
                 return ["T" + step[1:]]
             if step[0] == "T":
                 s, i = step[1:-2], step[-2]
-                need = [{"h": "lz", "dh": "ldz"}[s] + i] if int(i) in EARLY else [s + i]
-                return need + freed()
+                made = [{"h": "lz", "dh": "ldz"}[s] + i] if i in RAW else among(s + i, "hd" + i)
+                return made + freed()
             if step.startswith("dh"):
                 i = step[2]
-                return ["d" + i, "T" + step] if int(i) in EARLY else ["d" + i, "ldz" + i]
+                return ["d" + i, "T" + step if i in RAW else "ldz" + i]
             if step[0] == "h":
-                return ["d" + step[1]]
+                return ["d" + step[-1], "ldz" + step[-1]] if step[1] == "d" else ["d" + step[-1]]
             i = step[1]
-            return ["Eh" + i + "0", "Eh" + i + "1"] if int(i) in EARLY else ["lz" + i]
+            return ["Eh" + i + "0", "Eh" + i + "1"] if i in RAW else ["lz" + i]
 
         def emit(step):
             if step.startswith("lz") or step.startswith("ldz"):
                 i = int(step[-1])
-                src = z if step.startswith("lz") else dz
-                t[step] = work.tile([P, F], BF16, name=step[:-1], tag=step[:-1], bufs=4)
-                nc.sync.dma_start(out=t[step][:], in_=src[i * P : (i + 1) * P, :])
+                s, src = (0, z) if step.startswith("lz") else (1, dz)
+                nc.sync.dma_start(out=raw_rows(step[-1])[:, s, :], in_=src[i * P : (i + 1) * P, :])
             elif step == "lb":
                 nc.sync.dma_start(out=vb_rows[0:4, :], in_=vb.bitcast(F32).rearrange("(j p) -> j p", p=P))
-            elif step == "B0":
-                nc.tensor.transpose(bank("t", step)[:, 0:P], vb_rows[:], ident[:])
-            elif step == "b0":
-                nc.scalar.copy(out=vb_cols[:], in_=t["B0"][:, 0:4])
-            elif step == "B1":
-                dst = bank("t", step)
-                for j in range(4):
-                    nc.tensor.transpose(dst[:, j * P : (j + 1) * P], vb_cols[:, j : j + 1].to_broadcast([P, P]), ident[:])
-            elif step == "b1":
-                nc.scalar.copy(out=vb_all[:].bitcast(F32), in_=t["B1"][:])
             elif step.startswith("lc"):
-                i = int(step[2])
-                t[step] = keep.tile([P, N], BF16, name=step)
-                nc.sync.dma_start(out=t[step][:], in_=c[i * P : (i + 1) * P, :])
+                first = int(step[2]) * C_TILES * P
+                rows = c[first : first + C_TILES * P, :].rearrange("(i p) n -> p i n", p=P)
+                nc.sync.dma_start(out=shared("rows", "c" + step[2], [P, C_TILES, N], BF16, 5)[:], in_=rows)
             elif step.startswith("lv"):
                 g, n = int(step[2]), int(step[3])
-                t[step] = work.tile([P, 4, HALF], BF16, name="lv", tag="lv", bufs=4)
-                rows = v2[g * 512 : (g + 1) * 512, n * HALF : (n + 1) * HALF]
-                nc.sync.dma_start(out=t[step][:], in_=rows.rearrange("(p j) n -> p j n", j=4))
+                rows = v2[g * K_PASS : (g + 1) * K_PASS, n * HALF : (n + 1) * HALF]
+                dst = shared("vrows", step[2:], [P, 4, HALF], BF16, 4)
+                nc.sync.dma_start(out=dst[:], in_=rows.rearrange("(p j) n -> p j n", j=4))
             elif step.startswith("lw"):
                 n = int(step[2])
                 if n == 0:
@@ -189,106 +201,154 @@ def tile_gauss_newton_output_side_s1_kernel(tc, z, dz, w2_words, w2_scales, v2, 
                 t[step] = keep.tile([P, PASSES, 2 * HALF], U8, name=step, align_bytes=64)
                 words = w2_words[:, :, 2 * HALF * n : 2 * HALF * (n + 1)].rearrange("g p b -> p g b")
                 nc.sync.dma_start(out=t[step][:].bitcast(I32), in_=words.bitcast(I32))
-            elif step.startswith("st"):
-                i, n = int(step[2]), int(step[3])
-                nc.sync.dma_start(out=out[i * P : (i + 1) * P, n * HALF : (n + 1) * HALF], in_=t["A" + step[2:]][:])
-            elif step[0] == "X":
-                n = int(step[2])
-                o = t["A" + step[1:]]
-                nc.vector.tensor_tensor(out=o[:], in0=o[:], in1=t["lc" + step[1]][:, n * HALF : (n + 1) * HALF], op=ALU.mult)
-            elif step[0] == "A":
-                n = int(step[2])
-                t[step] = work.tile([P, HALF], F32, name="res", tag="res", bufs=10)
-                nc.vector.tensor_tensor(
-                    out=t[step][:], in0=t["M" + step[1:]][:], in1=vb_all[:, n * HALF : (n + 1) * HALF], op=ALU.add
+            elif step[0] == "s":
+                i = step[2]
+                cols = slice(0, N) if step[1] == "w" else columns(i, step[3])
+                nc.sync.dma_start(out=out[int(i) * P : (int(i) + 1) * P, cols], in_=t["result" + i][:, cols])
+            elif step == "B0":
+                nc.tensor.transpose(bank("turn", step)[:, 0:P], vb_rows[:], ident[:])
+            elif step == "b0":
+                nc.scalar.copy(out=vb_cols[:], in_=t["B0"][:, 0:4])
+            elif step == "B1":
+                dst = bank("turn", step)
+                for j in range(4):
+                    nc.tensor.transpose(dst[:, j * P : (j + 1) * P], vb_cols[:, j : j + 1].to_broadcast([P, P]), ident[:])
+            elif step == "b1":
+                nc.scalar.copy(out=vb_all[:].bitcast(F32), in_=t["B1"][:])
+            elif step == "Z":
+                zeros = shared("vmixed", "zeros", [P, 4 * HALF], BF16, 3)
+                codes, scales = quantised("zeros", HALF)
+                nc.vector.memset(zeros[:].bitcast(I32), 0)
+                nc.vector.quantize_mx(out=codes[:].bitcast(FP8X4), scales=scales[:], in_=zeros[:])
+            elif step[0] == "W":
+                if "spare" not in t:
+                    tag = "sum%d" % (BANKS - 1)
+                    t["spare"] = psum.tile([P, 512], F32, name=tag, tag=tag)
+                codes, scales = t["zeros"]
+                nc.tensor.matmul_mx(
+                    out=t["spare"][:],
+                    lhsT=codes[:, 0:P].bitcast(FP8X4),
+                    lhsT_scale=scales[:, 0:P],
+                    rhs=codes[:].bitcast(FP8X4),
+                    rhs_scale=scales[:],
+                    start=True,
+                    stop=True,
                 )
+            elif step[0] in "XY":
+                i = step[1]
+                cols = slice(0, N) if step[0] == "Y" else columns(i, step[2])
+                factor = t["rowsc%d" % (int(i) // C_TILES)][:, int(i) % C_TILES, cols]
+                res = t["result" + i][:, cols]
+                nc.vector.tensor_tensor(out=res, in0=res, in1=factor, op=ALU.mult)
+            elif step[0] == "A":
+                i, n = step[1], min(step[2], "1")
+                cols = columns(i, step[2])
+                acc = t["M" + i + n][:, cols.start - int(n) * HALF : cols.stop - int(n) * HALF]
+                res = shared("result", i, [P, N], F32, 6)[:, cols]
+                nc.vector.tensor_tensor(out=res, in0=acc, in1=vb_all[:, cols], op=ALU.add)
             elif step[0] == "M":
-                key, n, g = step[:3], int(step[2]), int(step[4])
+                i, n, kind, g = step[1], int(step[2]), step[3], int(step[4])
+                key = step[:3]
                 opening = key not in t
-                acc = bank("a", key) if opening else t[key]
-                t[key + "count"] = t.get(key + "count", 0) + 1
-                codes, scales = t[("Qdh" if step[3] == "w" else "Qh") + step[1]]
-                if step[3] == "w":
+                acc = bank("sum", key) if opening else t[key]
+                t[key + "passes"] = t.get(key + "passes", 0) + 1
+                codes, scales = t["act" + i]
+                first = side["dh" if kind == "w" else "h"] * (F // 4) + g * P
+                if kind == "w":
                     rhs = t["lw" + step[2]][:, g, :].bitcast(FP4X4)
                     rhs_scale = w_scales[:, g, n * HALF : (n + 1) * HALF]
                 else:
-                    v_codes, v_scales = t["Qv" + step[4] + step[2]]
+                    v_codes, v_scales = t["v" + step[4] + step[2]]
                     rhs, rhs_scale = v_codes[:].bitcast(FP8X4), v_scales[:]
                 nc.tensor.matmul_mx(
                     out=acc[:],
-                    lhsT=codes[:, g * P : (g + 1) * P].bitcast(FP8X4),
-                    lhsT_scale=scales[:, g * P : (g + 1) * P],
+                    lhsT=codes[:, first : first + P].bitcast(FP8X4),
+                    lhsT_scale=scales[:, first : first + P],
                     rhs=rhs,
                     rhs_scale=rhs_scale,
                     start=opening,
-                    stop=t[key + "count"] == 2 * PASSES,
+                    stop=t[key + "passes"] == 2 * PASSES,
                 )
+            elif step.startswith("Qv"):
+                codes, scales = quantised("v" + step[2:], HALF)
+                nc.vector.quantize_mx(out=codes[:].bitcast(FP8X4), scales=scales[:], in_=t["vmixed" + step[2:]][:])
             elif step[0] == "Q":
-                src = t["I" + step[2:]] if step[1] == "v" else t["k" + step[1:]]
-                codes = keep.tile([P, 512], U32, name=step + "codes", align_bytes=64)
-                scales = keep.tile([P, 512], U8, name=step + "scales", align_bytes=64)
-                t[step] = (codes, scales)
-                nc.vector.quantize_mx(out=codes[:].bitcast(FP8X4), scales=scales[:], in_=src[:])
+                i = step[-1]
+                first, count = (0, 2) if step[1] == "b" else (side[step[1:-1]], 1)
+                codes, scales = quantised("act" + i, F // 2)
+                cols = slice(first * (F // 4), (first + count) * (F // 4))
+                src = k_tile(i)[:, first : first + count, :].rearrange("p s k -> p (s k)")
+                nc.vector.quantize_mx(out=codes[:, cols].bitcast(FP8X4), scales=scales[:, cols], in_=src)
             elif step[0] == "I":
-                t[step] = work.tile([P, 4 * HALF], BF16, name="vi", tag="vi", bufs=3, align_bytes=64)
+                dst = shared("vmixed", step[1:], [P, 4 * HALF], BF16, 3)
                 nc.scalar.copy(
-                    out=t[step][:].rearrange("p (c i j) -> p c j i", i=4, j=4),
-                    in_=t["lv" + step[1:]][:].rearrange("p j (c i) -> p c j i", i=4),
+                    out=dst[:].rearrange("p (c i j) -> p c j i", i=4, j=4),
+                    in_=t["vrows" + step[1:]][:].rearrange("p j (c i) -> p c j i", i=4),
                 )
             elif step[0] == "E":
-                j = int(step[-1])
-                words = k_tile("k" + step[1:-1])[:].bitcast(F32)[:, j * 512 : (j + 1) * 512]
+                s, i, j = step[1:-2], step[-2], int(step[-1])
+                words = k_tile(i)[:, side[s], :].bitcast(F32)[:, j * 512 : (j + 1) * 512]
                 nc.scalar.copy(
                     out=words.rearrange("p (r u) -> p r u", u=2),
                     in_=t["T" + step[1:]][:].rearrange("p (u r) -> p r u", u=2),
                 )
             elif step[0] == "T":
                 s, i, j = step[1:-2], step[-2], int(step[-1])
-                dst = bank("t", step)
+                dst = bank("turn", step)
                 for gg in range(2):
                     g = 2 * j + gg
                     for u in range(2):
-                        if int(i) in EARLY:
-                            words = t[{"h": "lz", "dh": "ldz"}[s] + i][:].bitcast(F32)
-                            src = words[:, 256 * g + u : 256 * (g + 1) : 2]
+                        if i in RAW:
+                            src = raw_rows(i)[:, side[s], :].bitcast(F32)[:, 256 * g + u : 256 * (g + 1) : 2]
                         else:
-                            words = t[s + i][:].bitcast(F32)
-                            src = words[:, 512 * u + P * g : 512 * u + P * (g + 1)]
+                            src = parted(i)[:, u, side[s], :].bitcast(F32)[:, P * g : P * (g + 1)]
                         nc.tensor.transpose(dst[:, 256 * u + P * gg : 256 * u + P * (gg + 1)], src, ident[:])
-            elif step.startswith("dh") and int(step[2]) in EARLY:
+            elif step.startswith("dh") and step[2] in RAW:
                 i, j = step[2], int(step[3])
                 cols = slice(j * 1024, (j + 1) * 1024)
                 nc.vector.tensor_tensor(
-                    out=k_tile("kdh" + i)[:, cols].rearrange("p (r u e) -> p r u e", u=2, e=2),
+                    out=k_tile(i)[:, 1, cols].rearrange("p (r u e) -> p r u e", u=2, e=2),
                     in0=t["T" + step][:].bitcast(BF16).rearrange("p (u r e) -> p r u e", u=2, e=2),
-                    in1=t["d" + i][:, cols].rearrange("p (r u e) -> p r u e", u=2, e=2),
+                    in1=t["slope" + i][:, cols].rearrange("p (r u e) -> p r u e", u=2, e=2),
                     op=ALU.mult,
                 )
-            elif step[0] == "h" and int(step[1]) in EARLY:
-                kt = t["kh" + step[1]]
-                nc.vector.tensor_tensor(out=kt[:], in0=kt[:], in1=t["d" + step[1]][:], op=ALU.mult)
+            elif step[0] == "h" and step[1] in RAW:
+                zt = k_tile(step[1])[:, 0, :]
+                nc.vector.tensor_tensor(out=zt, in0=zt, in1=t["slope" + step[1]][:], op=ALU.mult)
+            elif step.startswith("hd"):
+                i = step[2]
+                slope = t["slope" + i][:].rearrange("p (u w e) -> p u w e", u=2, e=2)
+                nc.vector.tensor_tensor(
+                    out=parted(i)[:].rearrange("p u s (w e) -> p u s w e", e=2),
+                    in0=raw_rows(i)[:].rearrange("p s (w u e) -> p u s w e", u=2, e=2),
+                    in1=slope.unsqueeze(2).to_broadcast([P, 2, 2, F // 4, 2]),
+                    op=ALU.mult,
+                )
             elif step[0] == "h" or step.startswith("dh"):
-                i = step[-1]
-                src = t[("lz" if step[0] == "h" else "ldz") + i]
-                t[step] = work.tile([P, F], BF16, name="perm", tag="perm", bufs=3)
-                nc.vector.tensor_tensor(out=split(t[step][:]), in0=paired(src[:]), in1=split(t["d" + i][:]), op=ALU.mult)
+                s, i = side[step[:-1]], step[-1]
+                nc.vector.tensor_tensor(
+                    out=parted(i)[:, :, s, :].rearrange("p u (w e) -> p u w e", e=2),
+                    in0=raw_rows(i)[:, s, :].rearrange("p (w u e) -> p u w e", u=2, e=2),
+                    in1=t["slope" + i][:].rearrange("p (u w e) -> p u w e", u=2, e=2),
+                    op=ALU.mult,
+                )
             else:
                 i = step[1]
-                t[step] = work.tile([P, F], BF16, name="slope", tag="slope", bufs=3)
-                if int(i) in EARLY:
-                    dst, src = t[step][:], t["kh" + i][:]
+                dst = shared("slope", i, [P, F], BF16, 3)[:]
+                if i in RAW:
+                    src = k_tile(i)[:, 0, :]
                 else:
-                    dst, src = split(t[step][:]), paired(t["lz" + i][:])
+                    dst = dst.rearrange("p (u w e) -> p u w e", u=2, e=2)
+                    src = raw_rows(i)[:, 0, :].rearrange("p (w u e) -> p u w e", u=2, e=2)
                 nc.vector.tensor_scalar(out=dst, in0=src, scalar1=0.0, scalar2=SLOPE, op0=ALU.is_gt, op1=ALU.max)
 
-        queues = [expand(text) for text in (TENSOR, SCALAR, VECTOR, SYNC)]
         at = [0] * len(queues)
         done = set()
-        while len(done) < sum(len(q) for q in queues):
+        while len(done) < len(every):
             before = len(done)
-            for e, q in enumerate(queues):
-                if at[e] < len(q) and all(n in done for n in needs(q[at[e]])):
-                    emit(q[at[e]])
-                    done.add(q[at[e]])
+            for e, queue in enumerate(queues):
+                if at[e] < len(queue) and all(need in done for need in needs(queue[at[e]])):
+                    emit(queue[at[e]])
+                    done.add(queue[at[e]])
                     at[e] += 1
             assert len(done) > before

from contextlib import ExitStack

import concourse.mybir as mybir
from concourse.masks import make_identity

M, F, N = 1024, 2048, 1024
SLOPE = 0.25
FLOPS = 2 * 2 * M * F * N

F32 = mybir.dt.float32
BF16 = mybir.dt.bfloat16
I32 = mybir.dt.int32
U32 = mybir.dt.uint32
U8 = mybir.dt.uint8
FP8X4 = mybir.dt.float8_e4m3fn_x4
FP4X4 = mybir.dt.float4_e2m1fn_x4
ALU = mybir.AluOpType

P = 128
K_PASS = 512
PASSES = F // K_PASS
HALF = 512
BANKS = 4
C_TILES = 4
LAST = "7"

RAW = "234"

SYNC = """
lz0 lz2 lb ldz0 lz1 ldz1 lz3 lw0 ldz2 lv00 ldz3 lv10 lz4 lv20 ldz4 lv30 lv01 lz5 lv11 lw1 ldz5 lv21
lz6 lv31 ldz6 lz7 ldz7 lc0 lc1 sw0 sw1 sw2 sw3 sw4 st60 st61 sw5 st70 st71 st72
"""
VECTOR = """
Z d0 h0 dh0 d1 h1 dh1 Qh0 d2 Qdh0 h2 Qb1 dh2 d3 Qb2 Qv00 h3 dh3 Qv10 d4 Qb3 dh4 Qv20 h4 Qv30 Qb4 A00
Qv01 A10 d5 A20 A30 Qv11 A40 hd5 d6 Qv21 d7 Qv31 hd6 hd7 A01 A11 Qb5 A21 Y0 Y1 A31 A41 Y2 Qb6 A50 Y3
Y4 Qb7 A60 X60 A51 A61 Y5 X61 A70 X70 A71 A72 X71 X72
"""
SCALAR = """
Eh0 Edh0 Eh2 b0 Eh1 Edh1 Eh3 b1 I00 I10 Eh4 I20 I30 I01 I11 I21 I31 Eb5 Eb6 Eb7
"""
TENSOR = """
W2 W2 W2 Th0 W2 Tdh0 Th2 B0 W2 Th1 Tdh1 W2 Th3 B1 W2 Tdh2 M0:0w Tdh3 M1:0w Th4 M012:0v0 M2:0w Tdh4
M3:0w M0123:0v1 M3:0v0 M0123:0v2 M0123:0v3 M4:0 M0:1w M1:1w M012:1v0 M2:1w Tb5 M3:1w M3:1v0
M0123:1v1 M0123:1v2 M0123:1v3 Tb6 M4:1 Tb7 M5:0 M5:1 M6:0 M6:1 M7:0 M7:1
"""


def expand(text):
    steps = []
    for word in text.split():
        if word[0] == "M":
            tiles, rest = word[1:].split(":")
            kinds = rest[1:2] or "wv"
            passes = rest[2:3] or "0123"
            steps.extend("M" + i + rest[0] + kind + g for i in tiles for kind in kinds for g in passes)
        elif word[0] == "W":
            steps.extend("W%d.%d" % (len(steps), k) for k in range(int(word[1:])))
        elif word[:2] in ("Tb", "Eb"):
            steps.extend(word[0] + s + word[2] + j for s in ("h", "dh") for j in "01")
        elif word[0] in "TE" or (word.startswith("dh") and word[2] in RAW):
            steps.extend([word + "0", word + "1"])
        else:
            steps.append(word)
    return steps


def columns(i, n):
    if i == LAST and n != "0":
        first = HALF + (int(n) - 1) * (HALF // 2)
        return slice(first, first + HALF // 2)
    return slice(int(n) * HALF, (int(n) + 1) * HALF)


def tile_gauss_newton_output_side_s1_kernel(tc, z, dz, w2_words, w2_scales, v2, vb, c, out):
    nc = tc.nc
    with ExitStack() as ctx:
        keep = ctx.enter_context(tc.tile_pool(name="keep", bufs=1))
        work = ctx.enter_context(tc.tile_pool(name="work", bufs=1))
        psum = ctx.enter_context(tc.psum_pool(name="psum", bufs=1))
        ctx.enter_context(tc.manual_schedule())

        ident = keep.tile([P, P], F32, name="ident")
        vb_rows = keep.tile([P, P], F32, name="vb_rows")
        vb_cols = keep.tile([P, 4], F32, name="vb_cols")
        vb_all = keep.tile([P, N], BF16, name="vb_all")
        w_scales = keep.tile([P, PASSES, N], U8, name="w_scales", align_bytes=64)
        make_identity(nc, ident[:])
        nc.gpsimd.memset(vb_rows[:], 0.0)
        nc.gpsimd.memset(w_scales[:].bitcast(I32), 0)

        queues = [expand(text) for text in (TENSOR, SCALAR, VECTOR, SYNC)]
        every = [step for queue in queues for step in queue]
        side = {"h": 0, "dh": 1}
        t = {}
        turn = {"turn": [], "sum": []}

        def bank(kind, key):
            turn[kind].append(key)
            tag = "%s%d" % (kind, (len(turn[kind]) - 1) % BANKS)
            t[key] = psum.tile([P, 512], F32, name=tag, tag=tag)
            return t[key]

        def shared(tag, i, shape, dtype, bufs):
            if tag + i not in t:
                t[tag + i] = work.tile(shape, dtype, name=tag, tag=tag, bufs=bufs, align_bytes=64)
            return t[tag + i]

        def raw_rows(i):
            return shared("rows", i, [P, 2, F], BF16, 5)

        def k_tile(i):
            return shared("ktile", i, [P, 2, F], BF16, 4)

        def parted(i):
            return shared("parted", i, [P, 2, 2, F // 2], BF16, 2)

        def quantised(key, width):
            if key not in t:
                codes = keep.tile([P, width], U32, name=key + "codes", align_bytes=64)
                scales = keep.tile([P, width], U8, name=key + "scales", align_bytes=64)
                t[key] = (codes, scales)
            return t[key]

        def among(*steps):
            return [step for step in steps if step in every]

        def freed():
            if len(turn["turn"]) < BANKS:
                return []
            old = turn["turn"][-BANKS]
            return among("b" + old[1:], "E" + old[1:], old[1:])

        def needs(step):
            if step[0] == "l" or step == "Z":
                return []
            if step[0] == "W":
                return ["Z"]
            if step[0] == "B":
                return [{"0": "lb", "1": "b0"}[step[1]]] + freed()
            if step[0] == "b":
                return ["B" + step[1]]
            if step[0] == "s":
                return among("X" + step[2:], "Y" + step[2:])
            if step[0] in "XY":
                i = step[1]
                return ["lc%d" % (int(i) // C_TILES)] + (["A" + step[1:]] if step[0] == "X" else ["A" + i + "0", "A" + i + "1"])
            if step[0] == "A":
                key = "M" + step[1] + min(step[2], "1")
                return ["b1"] + [key + kind + g for kind in "wv" for g in "0123"]
            if step[0] == "M":
                i, n, kind, g = step[1:]
                need = among("Qb" + i, "Qdh" + i) + ["lw" + n] if kind == "w" else among("Qb" + i, "Qh" + i) + ["Qv" + g + n]
                if step[:3] not in t and len(turn["sum"]) >= BANKS:
                    need.append("A" + turn["sum"][-BANKS][1:])
                return need
            if step.startswith("Qv"):
                return ["I" + step[2:]]
            if step[0] == "I":
                return ["lv" + step[1:]]
            if step[0] == "Q":
                i = step[-1]
                sides = ("h", "dh") if step[1] == "b" else (step[1:-1],)
                makers = [s + i + j for s in sides for j in ("", "0", "1")]
                return among(*makers) if i in RAW else among(*["E" + maker for maker in makers])
            if step[0] == "E":
                return ["T" + step[1:]]
            if step[0] == "T":
                s, i = step[1:-2], step[-2]
                made = [{"h": "lz", "dh": "ldz"}[s] + i] if i in RAW else among(s + i, "hd" + i)
                return made + freed()
            if step.startswith("dh"):
                i = step[2]
                return ["d" + i, "T" + step if i in RAW else "ldz" + i]
            if step[0] == "h":
                return ["d" + step[-1], "ldz" + step[-1]] if step[1] == "d" else ["d" + step[-1]]
            i = step[1]
            return ["Eh" + i + "0", "Eh" + i + "1"] if i in RAW else ["lz" + i]

        def emit(step):
            if step.startswith("lz") or step.startswith("ldz"):
                i = int(step[-1])
                s, src = (0, z) if step.startswith("lz") else (1, dz)
                nc.sync.dma_start(out=raw_rows(step[-1])[:, s, :], in_=src[i * P : (i + 1) * P, :])
            elif step == "lb":
                nc.sync.dma_start(out=vb_rows[0:4, :], in_=vb.bitcast(F32).rearrange("(j p) -> j p", p=P))
            elif step.startswith("lc"):
                first = int(step[2]) * C_TILES * P
                rows = c[first : first + C_TILES * P, :].rearrange("(i p) n -> p i n", p=P)
                nc.sync.dma_start(out=shared("rows", "c" + step[2], [P, C_TILES, N], BF16, 5)[:], in_=rows)
            elif step.startswith("lv"):
                g, n = int(step[2]), int(step[3])
                rows = v2[g * K_PASS : (g + 1) * K_PASS, n * HALF : (n + 1) * HALF]
                dst = shared("vrows", step[2:], [P, 4, HALF], BF16, 4)
                nc.sync.dma_start(out=dst[:], in_=rows.rearrange("(p j) n -> p j n", j=4))
            elif step.startswith("lw"):
                n = int(step[2])
                if n == 0:
                    for q in range(4):
                        rows = w2_scales[:, 4 * q : 4 * q + 4, :].rearrange("g r n -> r g n")
                        nc.sync.dma_start(out=w_scales[32 * q : 32 * q + 4, :, :].bitcast(I32), in_=rows.bitcast(I32))
                t[step] = keep.tile([P, PASSES, 2 * HALF], U8, name=step, align_bytes=64)
                words = w2_words[:, :, 2 * HALF * n : 2 * HALF * (n + 1)].rearrange("g p b -> p g b")
                nc.sync.dma_start(out=t[step][:].bitcast(I32), in_=words.bitcast(I32))
            elif step[0] == "s":
                i = step[2]
                cols = slice(0, N) if step[1] == "w" else columns(i, step[3])
                nc.sync.dma_start(out=out[int(i) * P : (int(i) + 1) * P, cols], in_=t["result" + i][:, cols])
            elif step == "B0":
                nc.tensor.transpose(bank("turn", step)[:, 0:P], vb_rows[:], ident[:])
            elif step == "b0":
                nc.scalar.copy(out=vb_cols[:], in_=t["B0"][:, 0:4])
            elif step == "B1":
                dst = bank("turn", step)
                for j in range(4):
                    nc.tensor.transpose(dst[:, j * P : (j + 1) * P], vb_cols[:, j : j + 1].to_broadcast([P, P]), ident[:])
            elif step == "b1":
                nc.scalar.copy(out=vb_all[:].bitcast(F32), in_=t["B1"][:])
            elif step == "Z":
                zeros = shared("vmixed", "zeros", [P, 4 * HALF], BF16, 3)
                codes, scales = quantised("zeros", HALF)
                nc.vector.memset(zeros[:].bitcast(I32), 0)
                nc.vector.quantize_mx(out=codes[:].bitcast(FP8X4), scales=scales[:], in_=zeros[:])
            elif step[0] == "W":
                if "spare" not in t:
                    tag = "sum%d" % (BANKS - 1)
                    t["spare"] = psum.tile([P, 512], F32, name=tag, tag=tag)
                codes, scales = t["zeros"]
                nc.tensor.matmul_mx(
                    out=t["spare"][:],
                    lhsT=codes[:, 0:P].bitcast(FP8X4),
                    lhsT_scale=scales[:, 0:P],
                    rhs=codes[:].bitcast(FP8X4),
                    rhs_scale=scales[:],
                    start=True,
                    stop=True,
                )
            elif step[0] in "XY":
                i = step[1]
                cols = slice(0, N) if step[0] == "Y" else columns(i, step[2])
                factor = t["rowsc%d" % (int(i) // C_TILES)][:, int(i) % C_TILES, cols]
                res = t["result" + i][:, cols]
                nc.vector.tensor_tensor(out=res, in0=res, in1=factor, op=ALU.mult)
            elif step[0] == "A":
                i, n = step[1], min(step[2], "1")
                cols = columns(i, step[2])
                acc = t["M" + i + n][:, cols.start - int(n) * HALF : cols.stop - int(n) * HALF]
                res = shared("result", i, [P, N], F32, 6)[:, cols]
                nc.vector.tensor_tensor(out=res, in0=acc, in1=vb_all[:, cols], op=ALU.add)
            elif step[0] == "M":
                i, n, kind, g = step[1], int(step[2]), step[3], int(step[4])
                key = step[:3]
                opening = key not in t
                acc = bank("sum", key) if opening else t[key]
                t[key + "passes"] = t.get(key + "passes", 0) + 1
                codes, scales = t["act" + i]
                first = side["dh" if kind == "w" else "h"] * (F // 4) + g * P
                if kind == "w":
                    rhs = t["lw" + step[2]][:, g, :].bitcast(FP4X4)
                    rhs_scale = w_scales[:, g, n * HALF : (n + 1) * HALF]
                else:
                    v_codes, v_scales = t["v" + step[4] + step[2]]
                    rhs, rhs_scale = v_codes[:].bitcast(FP8X4), v_scales[:]
                nc.tensor.matmul_mx(
                    out=acc[:],
                    lhsT=codes[:, first : first + P].bitcast(FP8X4),
                    lhsT_scale=scales[:, first : first + P],
                    rhs=rhs,
                    rhs_scale=rhs_scale,
                    start=opening,
                    stop=t[key + "passes"] == 2 * PASSES,
                )
            elif step.startswith("Qv"):
                codes, scales = quantised("v" + step[2:], HALF)
                nc.vector.quantize_mx(out=codes[:].bitcast(FP8X4), scales=scales[:], in_=t["vmixed" + step[2:]][:])
            elif step[0] == "Q":
                i = step[-1]
                first, count = (0, 2) if step[1] == "b" else (side[step[1:-1]], 1)
                codes, scales = quantised("act" + i, F // 2)
                cols = slice(first * (F // 4), (first + count) * (F // 4))
                src = k_tile(i)[:, first : first + count, :].rearrange("p s k -> p (s k)")
                nc.vector.quantize_mx(out=codes[:, cols].bitcast(FP8X4), scales=scales[:, cols], in_=src)
            elif step[0] == "I":
                dst = shared("vmixed", step[1:], [P, 4 * HALF], BF16, 3)
                nc.scalar.copy(
                    out=dst[:].rearrange("p (c i j) -> p c j i", i=4, j=4),
                    in_=t["vrows" + step[1:]][:].rearrange("p j (c i) -> p c j i", i=4),
                )
            elif step[0] == "E":
                s, i, j = step[1:-2], step[-2], int(step[-1])
                words = k_tile(i)[:, side[s], :].bitcast(F32)[:, j * 512 : (j + 1) * 512]
                nc.scalar.copy(
                    out=words.rearrange("p (r u) -> p r u", u=2),
                    in_=t["T" + step[1:]][:].rearrange("p (u r) -> p r u", u=2),
                )
            elif step[0] == "T":
                s, i, j = step[1:-2], step[-2], int(step[-1])
                dst = bank("turn", step)
                for gg in range(2):
                    g = 2 * j + gg
                    for u in range(2):
                        if i in RAW:
                            src = raw_rows(i)[:, side[s], :].bitcast(F32)[:, 256 * g + u : 256 * (g + 1) : 2]
                        else:
                            src = parted(i)[:, u, side[s], :].bitcast(F32)[:, P * g : P * (g + 1)]
                        nc.tensor.transpose(dst[:, 256 * u + P * gg : 256 * u + P * (gg + 1)], src, ident[:])
            elif step.startswith("dh") and step[2] in RAW:
                i, j = step[2], int(step[3])
                cols = slice(j * 1024, (j + 1) * 1024)
                nc.vector.tensor_tensor(
                    out=k_tile(i)[:, 1, cols].rearrange("p (r u e) -> p r u e", u=2, e=2),
                    in0=t["T" + step][:].bitcast(BF16).rearrange("p (u r e) -> p r u e", u=2, e=2),
                    in1=t["slope" + i][:, cols].rearrange("p (r u e) -> p r u e", u=2, e=2),
                    op=ALU.mult,
                )
            elif step[0] == "h" and step[1] in RAW:
                zt = k_tile(step[1])[:, 0, :]
                nc.vector.tensor_tensor(out=zt, in0=zt, in1=t["slope" + step[1]][:], op=ALU.mult)
            elif step.startswith("hd"):
                i = step[2]
                slope = t["slope" + i][:].rearrange("p (u w e) -> p u w e", u=2, e=2)
                nc.vector.tensor_tensor(
                    out=parted(i)[:].rearrange("p u s (w e) -> p u s w e", e=2),
                    in0=raw_rows(i)[:].rearrange("p s (w u e) -> p u s w e", u=2, e=2),
                    in1=slope.unsqueeze(2).to_broadcast([P, 2, 2, F // 4, 2]),
                    op=ALU.mult,
                )
            elif step[0] == "h" or step.startswith("dh"):
                s, i = side[step[:-1]], step[-1]
                nc.vector.tensor_tensor(
                    out=parted(i)[:, :, s, :].rearrange("p u (w e) -> p u w e", e=2),
                    in0=raw_rows(i)[:, s, :].rearrange("p (w u e) -> p u w e", u=2, e=2),
                    in1=t["slope" + i][:].rearrange("p (u w e) -> p u w e", u=2, e=2),
                    op=ALU.mult,
                )
            else:
                i = step[1]
                dst = shared("slope", i, [P, F], BF16, 3)[:]
                if i in RAW:
                    src = k_tile(i)[:, 0, :]
                else:
                    dst = dst.rearrange("p (u w e) -> p u w e", u=2, e=2)
                    src = raw_rows(i)[:, 0, :].rearrange("p (w u e) -> p u w e", u=2, e=2)
                nc.vector.tensor_scalar(out=dst, in0=src, scalar1=0.0, scalar2=SLOPE, op0=ALU.is_gt, op1=ALU.max)

        at = [0] * len(queues)
        done = set()
        while len(done) < len(every):
            before = len(done)
            for e, queue in enumerate(queues):
                if at[e] < len(queue) and all(need in done for need in needs(queue[at[e]])):
                    emit(queue[at[e]])
                    done.add(queue[at[e]])
                    at[e] += 1
            assert len(done) > before
